import numpy as np
CORES = [33,161,289,417,57,185,313,441]
N = 8
T, SQ = 1024, 512
def entries(a): return a.T.reshape(-1)
def pack(v, P): return np.ascontiguousarray(np.asarray(v, np.int32).reshape(-1, P).T)
def lists(rng, how):
    d = np.concatenate([[0], rng.integers(1 - SQ // 2, SQ // 2, N - 1), [int(rng.integers(1 - SQ // 2, 1))]])
    if how == "lag": d[1:] = -SQ
    if how == "lead": d[1:N] = SQ; d[N] = 0
    if how == "runs": m = int(rng.integers(1, N - 2)); d[m] = -abs(d[m]); d[m + 1] = d[m] + SQ; d[m + 2] = d[m]
    if how == "skew": t = int(rng.integers(2, N - 1)); d[1:] = rng.integers(SQ // 2 + 1, SQ - 1, N); d[t + 1:] *= -1; d[t] = d[t - 1] + d[t + 1]
    n = SQ + np.diff(d)
    F = np.zeros((N, T), np.int64)
    for r in range(N):
        o = rng.permutation(T)
        if how == "runs": o = (T // 16 * rng.permutation(16)[:, None] + np.arange(T // 16)).reshape(-1)
        if how == "skew": o = np.concatenate([[0, T - 1], 1 + rng.permutation(T - 2)])
        F[r, o[:n[r]]] = 1
    return {"fl": np.stack([pack(f, 16) for f in F])}
def setup_inputs(rng):
    return dict({"x": rng.standard_normal((N, 128, T), dtype=np.float32), "st": rng.standard_normal((N, 128, SQ), dtype=np.float32)}, **lists(rng, "uniform"))
def setup_inputs_lag(rng):
    d = setup_inputs(rng); d.update(lists(rng, "lag"))
    for k in ("x", "st"): d[k] = (d[k].astype(np.float32) * 1048576.0).astype(d[k].dtype)
    return d
def setup_inputs_lead(rng):
    d = setup_inputs(rng); d.update(lists(rng, "lead"))
    for k in ("x", "st"): d[k] = (d[k].astype(np.float32) * (1 / 1024.0)).astype(d[k].dtype)
    return d
def setup_inputs_runs(rng):
    d = setup_inputs(rng); d.update(lists(rng, "runs"))
    return d
def setup_inputs_skew(rng):
    d = setup_inputs(rng); d.update(lists(rng, "skew"))
    return d
def check_inputs(x):
    bad = []
    if x["fl"].min() < 0 or x["fl"].max() >= 2: bad.append("fl out of range")
    if int(x["fl"].sum()) > N * SQ: bad.append("more flags than the stream has columns")
    c = np.concatenate([[0], np.cumsum([int(a.sum()) for a in x["fl"]])])
    if any(c[r] < (r - 1) * SQ or c[r + 1] > (r + 2) * SQ for r in range(N)): bad.append("a rank's share of the stream reaches beyond its neighbours' parts")
    return bad
def reference(x, st, fl):
    S = np.concatenate(list(st), axis=1); X = np.concatenate(list(x), axis=1)
    F = np.concatenate([entries(f) for f in fl]) > 0; c = np.cumsum(F) - F
    Y = np.where(F[None, :], S[:, np.minimum(c, N * SQ - 1)], X)
    return {"y": np.stack([Y[:, T * r:T * r + T] for r in range(N)])}

@@ -1,0 +1,277 @@
+import numpy as np
+from concourse.bass import DstId, RemoteDMATransfer
+from concourse.mybir import dt, AluOpType, AxisListType, ActivationFunctionType
+
+TC = 1024
+SQ = 512
+NR = 8
+BIG = 8192.0
+
+SCRATCH = {
+    "win": ("sbuf", [128, TC + 3 * SQ], "float32"),
+    "yb": ("sbuf", [128, TC], "float32"),
+    "rb": ("sbuf", [128, SQ], "float32"),
+    "fd": ("dram", [NR, 128, 8], "int32"),
+    "fo": ("sbuf", [16, 64], "int32"),
+    "fp": ("sbuf", [128, 64], "int32"),
+    "fob": ("sbuf", [16, 64], "bfloat16"),
+    "fpb": ("sbuf", [128, 64], "bfloat16"),
+    "ones": ("sbuf", [128, 128], "bfloat16"),
+    "neg": ("sbuf", [16, 128], "bfloat16"),
+    "big": ("sbuf", [16, 128], "bfloat16"),
+    "lm": ("sbuf", [16, 128], "bfloat16"),
+    "br": ("sbuf", [16, 128], "bfloat16"),
+    "jv": ("sbuf", [128, 64], "int32"),
+    "ja": ("sbuf", [128, 64], "int32"),
+    "jb": ("sbuf", [128, 64], "int32"),
+    "jj": ("sbuf", [128, 64], "float32"),
+    "ee": ("sbuf", [128, 65], "float32"),
+    "d0": ("sbuf", [128, 128], "float32"),
+    "us": ("sbuf", [128, 128], "float32"),
+    "of": ("sbuf", [128, 64], "float32"),
+    "off": ("sbuf", [128, 64], "uint16"),
+    "psa": ("psum", [128, 512], "float32"),
+    "psb": ("psum", [128, 512], "float32"),
+}
+SEMAPHORES = (["f%d" % q for q in range(NR)]
+              + ["ldfd", "ldfo", "ldst", "ldx", "ldfp", "darr", "rarr", "snt", "msk", "mone", "mz", "aff", "iot",
+                 "vj1", "vj2", "vj", "vfo", "pe1", "pe2", "vee", "vd0", "vfp", "pe3", "vus", "vof", "voff",
+                 "gv", "gs", "sty0", "sty1"])
+
+PLANS = {}
+
+
+def bits(mask):
+    return [1 << i for i in range(16) if (mask >> i) & 1]
+
+
+def part(mask, k, n):
+    b = bits(mask)
+    m = len(b) // n
+    return sum(b[k * m:(k + 1) * m])
+
+
+def make_plan(cores, topo):
+    total = topo.CORES_PER_HOST * (1 + max(topo.host(c) for c in cores))
+    place = {}
+    for k in range(total):
+        place.setdefault((topo.host(k), topo.chip(k)), []).append(k)
+    same = lambda a: place[(topo.host(a), topo.chip(a))]
+    n = len(cores)
+    used = {}
+
+    def pick(cand):
+        b = min(cand, key=lambda k: (used.get(k, 0), cand.index(k)))
+        used[b] = used.get(b, 0) + 1
+        return b
+
+    def base(r, p):
+        return TC + SQ * (p - max(r - 1, 0))
+
+    data, relay = {}, {}
+    H = SQ // 2
+    for s in range(n):
+        first, second = [], []
+        cs = cores[s]
+        for d in (s - 1, s + 1):
+            if not 0 <= d < n:
+                continue
+            cd = cores[d]
+            so, do = base(s, s), base(d, s)
+            if topo.may_write(cs, cd) and topo.same_plane(cs, cd):
+                second.append((cd, "win", so, "win", do, SQ, topo.mask(cs, cd)))
+                continue
+            mates = [k for k in same(cs) if k not in cores and topo.may_write(k, cd)]
+            if topo.may_write(cs, cd):
+                first.append((cd, "win", so, "win", do, H, topo.mask(cs, cd)))
+                hs = [pick([k for k in mates if topo.die(k) != topo.die(cs)])]
+                piece = [(hs[0], H)]
+                on = topo.mask(cs, hs[0]) & ~topo.mask(cs, cd)
+            else:
+                hs = [pick([k for k in mates if topo.die(k) == e]) for e in (0, 1)]
+                piece = [(hs[0], 0), (hs[1], H)]
+                on = topo.mask(cs, hs[0])
+            for i, (h, o) in enumerate(piece):
+                first.append((h, "win", so + o, "rb", 0, H, part(on, i, len(piece))))
+                relay[h] = (cd, "rb", 0, "win", do + o, H, topo.mask(h, cd))
+        data[cs] = [c for c in (first, second) if c]
+    for h in relay:
+        data[h] = [[relay[h]]]
+
+    flags, listed = {}, {}
+    for q in range(n):
+        cq = cores[q]
+        direct, hops = [], {}
+        for r in range(q + 1, n):
+            cr = cores[r]
+            if topo.may_write(cq, cr):
+                direct.append(cr)
+                continue
+            via = [h for h in hops if topo.may_write(h, cr)]
+            if via:
+                h = via[0]
+            else:
+                own = [k for k in same(cq) if k not in cores and topo.may_write(k, cr)]
+                far = [k for c in cores for k in same(c) if k not in cores and topo.may_write(cq, k)
+                       and topo.may_write(k, cr)]
+                rest = [cores[t] for t in range(r, n) if not topo.may_write(cq, cores[t])]
+                h = min(own or far, key=lambda k: (-sum(topo.may_write(k, t) for t in rest), listed.get(k, 0),
+                                                   k not in relay))
+                listed[h] = listed.get(h, 0) + 1
+            hops.setdefault(h, []).append(cr)
+        if direct or hops:
+            flags.setdefault(cq, []).append((q, direct + list(hops)))
+        for h in hops:
+            flags.setdefault(h, []).append((q, hops[h]))
+    return flags, data, relay
+
+
+def rank_program(g, core, T, topo):
+    cores = list(T.cores)
+    if "p" not in PLANS:
+        PLANS["p"] = make_plan(cores, topo)
+    flags, data, relay = PLANS["p"]
+    rank = T.rank_of(core)
+    if rank is None and core not in flags and core not in data:
+        return
+    S = T.sem
+    sent = [0]
+
+    def fmask(c, dsts):
+        m = topo.mask(c, dsts[0])
+        for d in dsts[1:]:
+            m &= topo.mask(c, d)
+        return part(m, 0, len(bits(m)) // 8)
+
+    def dstid(d):
+        rid, pid = topo.addr(d, core)
+        return DstId(rid=rid, pnc=pid)
+
+    def nbits(m):
+        return len(bits(m))
+
+    def send_flags(q, dsts):
+        m = fmask(core, dsts)
+        g.remote_dma_fused([RemoteDMATransfer(dst_ids=[dstid(d) for d in dsts], dma_engine_mask=m,
+                                              remote_sem=S["f%d" % q], srcs=[T.fd[q]],
+                                              dsts=[T.fd[q] for d in dsts])], local_sem=S.snt)
+        sent[0] += nbits(m)
+
+    def send_data(call):
+        tr = []
+        for (d, sb, sc, db, dc, w, m) in call:
+            tr.append(RemoteDMATransfer(dst_ids=[dstid(d)], dma_engine_mask=m,
+                                        remote_sem=S["darr" if db == "win" else "rarr"],
+                                        srcs=[T[sb][:, sc:sc + w]], dsts=[T[db][:, dc:dc + w]]))
+            sent[0] += nbits(m)
+        g.remote_dma_fused(tr, local_sem=S.snt)
+
+    def flag_count(q, me):
+        for c in flags:
+            for (qq, dsts) in flags[c]:
+                if qq == q and me in dsts:
+                    return nbits(fmask(c, dsts))
+        return 0
+
+    def landing(me, buf):
+        return sum(nbits(t[6]) for c in data for call in data[c] for t in call if t[0] == me and t[3] == buf)
+
+    if rank is None:
+        for (q, dsts) in flags.get(core, []):
+            g.wait_ge(S["f%d" % q], flag_count(q, core))
+            send_flags(q, dsts)
+        if core in data:
+            g.wait_ge(S.rarr, landing(core, "rb"))
+            for call in data[core]:
+                send_data(call)
+        g.wait_ge(S.snt, sent[0])
+        return
+
+    r = rank
+    n = len(cores)
+    first = max(r - 1, 0)
+    parts = min(r + 1, n - 1) - first + 1
+    W = TC + SQ * parts
+    own = TC + SQ * (r - first)
+    lo = 64 if r == 0 else 0
+    add, mx = AluOpType.add, AluOpType.max
+
+    g.sync.dma_start(T.win[:, own:own + SQ], T.st[:]).then_inc(S.ldst, 16)
+    g.sync.dma_start(T.win[:, 0:TC], T.x[:]).then_inc(S.ldx, 16)
+    if core in flags:
+        g.scalar.dma_start(T.fd[r], T.fl[:]).then_inc(S.ldfd, 16)
+    g.scalar.dma_start(T.fo[:], T.fl[:]).then_inc(S.ldfo, 16)
+
+    V = g.vector
+    V.memset(T.neg[:], -1.0).then_inc(S.msk, 1)
+    V.memset(T.big[:], BIG).then_inc(S.msk, 1)
+    V.memset(T.ones[:], 1.0).then_inc(S.mone, 1)
+    V.memset(T.ee[:, 0:1], 0.0).then_inc(S.mz, 1)
+    V.memset(T.d0[:, 0:64], 0.0).then_inc(S.mz, 1)
+    g.iota(T.jv[:], [[256, 64]], 0, 1).then_inc(S.iot, 1)
+    g.wait_ge(S.msk, 2)
+    g.affine_select(T.lm[:], T.neg[:], [[0, 8], [-1, 16]], AluOpType.is_ge, 0.0, 0, 1).then_inc(S.aff, 1)
+    g.affine_select(T.br[:], T.big[:], [[0, 8], [-1, 16]], AluOpType.is_equal, 0.0, 0, 1).then_inc(S.aff, 1)
+
+    for (q, dsts) in flags.get(core, []):
+        g.wait_ge(S.ldfd, 16)
+        send_flags(q, dsts)
+    g.wait_ge(S.ldst, 16)
+    for call in data[core]:
+        send_data(call)
+
+    V.wait_ge(S.iot, 1)
+    V.tensor_scalar(T.ja[:], T.jv[:], 15, None, AluOpType.bitwise_and).then_inc(S.vj1, 1)
+    V.tensor_scalar(T.jb[:], T.jv[:], 4, 1008, AluOpType.arith_shift_right, AluOpType.bitwise_and).then_inc(S.vj2, 1)
+    V.wait_ge(S.vj1, 1)
+    V.wait_ge(S.vj2, 1)
+    V.tensor_tensor(T.jj[:], T.ja[:], T.jb[:], add).then_inc(S.vj, 1)
+    V.wait_ge(S.ldfo, 16)
+    V.tensor_copy(T.fob[:], T.fo[:]).then_inc(S.vfo, 1)
+    P = g.tensor
+    P.wait_ge(S.mone, 1)
+    P.wait_ge(S.aff, 2)
+    P.wait_ge(S.vfo, 1)
+    P.matmul(T.psb[:, 0:64], T.lm[:], T.fob[:], True, False)
+    P.matmul(T.psb[:, 0:64], T.br[:], T.fob[:], False, True).then_inc(S.pe1, 1)
+    P.matmul(T.psa[:, 64:128], T.ones[0:16, :], T.fob[:], True, True).then_inc(S.pe2, 1)
+    V.wait_ge(S.pe1, 1)
+    V.tensor_scalar(T.ee[:, 1:65], T.psb[:, 0:64], float(TC - SQ * first) - BIG, None, add).then_inc(S.vee, 1)
+    V.wait_ge(S.vee, 1)
+    V.wait_ge(S.mz, 2)
+    V.tensor_tensor(T.d0[:, 64:128], T.ee[:, 1:65], T.ee[:, 0:64], AluOpType.subtract).then_inc(S.vd0, 1)
+
+    if r:
+        for q in range(r):
+            g.scalar.wait_ge(S["f%d" % q], flag_count(q, core))
+        g.scalar.dma_start(T.fp[0:16 * r, :], T.fd[0:r]).then_inc(S.ldfp, 16)
+        V.wait_ge(S.ldfp, 16)
+        V.tensor_copy(T.fpb[0:16 * r, :], T.fp[0:16 * r, :]).then_inc(S.vfp, 1)
+        P.wait_ge(S.vfp, 1)
+        P.matmul(T.psa[:, 0:64], T.ones[0:16 * r, :], T.fpb[0:16 * r, :], True, True).then_inc(S.pe3, 1)
+        V.wait_ge(S.pe3, 1)
+    V.wait_ge(S.pe2, 1)
+    V.wait_ge(S.vd0, 1)
+    V.tensor_tensor_scan(T.us[:, lo:128], T.d0[:, lo:128], T.psa[:, lo:128], 0.0, add, add).then_inc(S.vus, 1)
+    V.wait_ge(S.vus, 1)
+    V.wait_ge(S.vj, 1)
+    V.tensor_tensor(T.of[:], T.us[:, 64:128], T.jj[:], mx).then_inc(S.vof, 1)
+    V.wait_ge(S.vof, 1)
+    V.tensor_copy(T.off[:], T.of[:]).then_inc(S.voff, 1)
+
+    for Q in (V, g.scalar):
+        Q.wait_ge(S.voff, 1)
+        Q.wait_ge(S.ldst, 16)
+        Q.wait_ge(S.ldx, 16)
+        Q.wait_ge(S.darr, landing(core, "win"))
+    HT = TC // 2
+    V.tensor_copy(T.yb[:, 0:HT], T.win[:, 0:W].indirect(T.off[:, 0:32])).then_inc(S.gv, 1)
+    g.scalar.activation(T.yb[:, HT:TC], T.win[:, 0:W].indirect(T.off[:, 32:64]),
+                        ActivationFunctionType.Copy).then_inc(S.gs, 1)
+    g.sync.wait_ge(S.gv, 1)
+    g.sync.dma_start(T.y[:, 0:HT], T.yb[:, 0:HT]).then_inc(S.sty0, 16)
+    g.scalar.wait_ge(S.gs, 1)
+    g.scalar.dma_start(T.y[:, HT:TC], T.yb[:, HT:TC]).then_inc(S.sty1, 16)
+    g.sync.wait_ge(S.sty0, 16)
+    g.scalar.wait_ge(S.sty1, 16)
+    g.wait_ge(S.snt, sent[0])

@@ -6,16 +6,20 @@ TC = 1024
 SQ = 512
 NR = 8
 BIG = 8192.0
+LW = 8
+FIRST = 256
 
 SCRATCH = {
     "win": ("sbuf", [128, TC + 3 * SQ], "float32"),
     "yb": ("sbuf", [128, TC], "float32"),
-    "rb": ("sbuf", [128, SQ], "float32"),
-    "fd": ("dram", [NR, 128, 8], "int32"),
-    "fo": ("sbuf", [16, 64], "int32"),
+    "rb": ("sbuf", [128, SQ // 2], "float32"),
+    "fd": ("dram", [NR, 128, LW], "int32"),
+    "ls": ("sbuf", [128, LW * NR], "int32"),
+    "lb": ("sbuf", [128, LW * NR], "bfloat16"),
     "fp": ("sbuf", [128, 64], "int32"),
-    "fob": ("sbuf", [16, 64], "bfloat16"),
     "fpb": ("sbuf", [128, 64], "bfloat16"),
+    "fo": ("sbuf", [16, 64], "int32"),
+    "fob": ("sbuf", [16, 64], "bfloat16"),
     "ones": ("sbuf", [128, 128], "bfloat16"),
     "neg": ("sbuf", [16, 128], "bfloat16"),
     "big": ("sbuf", [16, 128], "bfloat16"),
@@ -26,17 +30,17 @@ SCRATCH = {
     "jb": ("sbuf", [128, 64], "int32"),
     "jj": ("sbuf", [128, 64], "float32"),
     "ee": ("sbuf", [128, 65], "float32"),
-    "d0": ("sbuf", [128, 128], "float32"),
-    "us": ("sbuf", [128, 128], "float32"),
+    "d0": ("sbuf", [128, 192], "float32"),
+    "us": ("sbuf", [128, 192], "float32"),
     "of": ("sbuf", [128, 64], "float32"),
     "off": ("sbuf", [128, 64], "uint16"),
     "psa": ("psum", [128, 512], "float32"),
     "psb": ("psum", [128, 512], "float32"),
 }
 SEMAPHORES = (["f%d" % q for q in range(NR)]
-              + ["ldfd", "ldfo", "ldst", "ldx", "ldfp", "darr", "rarr", "snt", "msk", "mone", "mz", "aff", "iot",
-                 "vj1", "vj2", "vj", "vfo", "pe1", "pe2", "vee", "vd0", "vfp", "pe3", "vus", "vof", "voff",
-                 "gv", "gs", "sty0", "sty1"])
+              + ["ldfd", "ldfo", "ldst", "ldx", "ldls", "darr", "rarr", "snt", "msk", "mone", "mz", "aff", "iot",
+                 "vj1", "vj2", "vj", "vfo", "pe1", "pe2", "vee", "vd0", "vfp", "vfq", "pe3", "pe4", "vus", "vof",
+                 "voff", "gv0", "gs0", "gv1", "gs1", "sty0", "sty1"])
 
 PLANS = {}
 
@@ -46,9 +50,7 @@ def bits(mask):
 
 
 def part(mask, k, n):
-    b = bits(mask)
-    m = len(b) // n
-    return sum(b[k * m:(k + 1) * m])
+    return sum(bits(mask)[k::n])
 
 
 def make_plan(cores, topo):
@@ -57,91 +59,117 @@ def make_plan(cores, topo):
     for k in range(total):
         place.setdefault((topo.host(k), topo.chip(k)), []).append(k)
     same = lambda a: place[(topo.host(a), topo.chip(a))]
+    rack = lambda k: topo.rack(topo.host(k))
     n = len(cores)
-    used = {}
+    H = SQ // 2
 
-    def pick(cand):
-        b = min(cand, key=lambda k: (used.get(k, 0), cand.index(k)))
-        used[b] = used.get(b, 0) + 1
-        return b
+    data, stream = {}, {}
 
     def base(r, p):
         return TC + SQ * (p - max(r - 1, 0))
 
-    data, relay = {}, {}
-    H = SQ // 2
+    def idle(c):
+        return [k for k in same(c) if k not in cores and k not in stream]
+
     for s in range(n):
-        first, second = [], []
+        relayed, plane = [], []
         cs = cores[s]
+
+        def via(h, d, o, m):
+            stream[h] = s
+            data[h] = [[(cores[d], "rb", 0, "win", base(d, s) + o, H, topo.mask(h, cores[d]))]]
+            return (h, "win", base(s, s) + o, "rb", 0, H, m)
+
         for d in (s - 1, s + 1):
             if not 0 <= d < n:
                 continue
             cd = cores[d]
             so, do = base(s, s), base(d, s)
             if topo.may_write(cs, cd) and topo.same_plane(cs, cd):
-                second.append((cd, "win", so, "win", do, SQ, topo.mask(cs, cd)))
-                continue
-            mates = [k for k in same(cs) if k not in cores and topo.may_write(k, cd)]
-            if topo.may_write(cs, cd):
-                first.append((cd, "win", so, "win", do, H, topo.mask(cs, cd)))
-                hs = [pick([k for k in mates if topo.die(k) != topo.die(cs)])]
-                piece = [(hs[0], H)]
-                on = topo.mask(cs, hs[0]) & ~topo.mask(cs, cd)
+                plane.append([(cd, "win", so, "win", do, SQ, topo.mask(cs, cd))])
+            elif topo.may_write(cs, cd):
+                h = [k for k in idle(cs) if topo.may_write(k, cd) and topo.die(k) != topo.die(cs)
+                     and any(topo.may_write(k, c) for c in cores if not topo.may_write(cs, c))][0]
+                relayed.append([via(h, d, H, topo.mask(cs, h) & ~topo.mask(cs, cd)),
+                                (cd, "win", so, "win", do, H, topo.mask(cs, cd))])
             else:
-                hs = [pick([k for k in mates if topo.die(k) == e]) for e in (0, 1)]
-                piece = [(hs[0], 0), (hs[1], H)]
-                on = topo.mask(cs, hs[0])
-            for i, (h, o) in enumerate(piece):
-                first.append((h, "win", so + o, "rb", 0, H, part(on, i, len(piece))))
-                relay[h] = (cd, "rb", 0, "win", do + o, H, topo.mask(h, cd))
-        data[cs] = [c for c in (first, second) if c]
-    for h in relay:
-        data[h] = [[relay[h]]]
+                h0, h1 = [[k for k in idle(cs) if topo.may_write(k, cd) and topo.die(k) == e][0] for e in (0, 1)]
+                on = topo.mask(cs, h0)
+                relayed.append([via(h0, d, 0, part(on, 1, 2)), via(h1, d, H, part(on, 0, 2))])
+        data[cs] = relayed + plane
 
-    flags, listed = {}, {}
+    hops, jobs = {}, set()
+    held = set()
+    last = n - 1
+
+    def give(q, h, r):
+        hops[(q, h)] = r
+        jobs.add(h)
+
+    def beside(k, r):
+        return topo.mates(k, place[(topo.host(k), topo.chip(cores[r]))][0])
+
+    odd = [h for h in stream if not topo.may_write(cores[stream[h]], data[h][0][0][0])]
+    for h in odd:
+        can = [q for q in range(last) if (q, last) not in held and topo.may_write(cores[q], h)
+               and topo.may_write(h, cores[last])]
+        can.sort(key=lambda q: (q != stream[h], rack(cores[q]) != rack(h), -q))
+        if can:
+            give(can[0], h, last)
+            held.add((can[0], last))
     for q in range(n):
         cq = cores[q]
-        direct, hops = [], {}
-        for r in range(q + 1, n):
+        todo = [r for r in range(q + 1, n) if (q, r) not in held]
+        for h in [h for h in stream if stream[h] == q and h not in jobs]:
+            goal = topo.host(data[h][0][0][0])
+            can = [r for r in todo if topo.may_write(h, cores[r])]
+            can.sort(key=lambda r: (topo.host(cores[r]) != goal, topo.may_write(cq, cores[r])))
+            if can:
+                give(q, h, can[0])
+                todo.remove(can[0])
+        for r in todo:
             cr = cores[r]
-            if topo.may_write(cq, cr):
-                direct.append(cr)
-                continue
-            via = [h for h in hops if topo.may_write(h, cr)]
-            if via:
-                h = via[0]
+            cand = [k for p in place.values() for k in p if k not in cores and k not in stream and k not in jobs
+                    and topo.may_write(cq, k) and topo.may_write(k, cr)]
+            other = [k for k in cand if topo.die(k) != topo.die(cq)]
+            if topo.chip(cq) != topo.chip(cr):
+                if topo.host(cr) == topo.host(cq):
+                    good = [k for k in other if topo.mates(k, cr)]
+                else:
+                    good = [k for k in other if k in same(cq) and not any(h in same(cq) for h in odd)]
+                    good = good or [k for k in other if topo.mates(k, cr)]
+                good = good or [k for k in other if beside(k, r) and rack(k) == rack(cr)]
+                good = good or [k for k in cand if beside(k, r) and rack(k) == rack(cq)]
             else:
-                own = [k for k in same(cq) if k not in cores and topo.may_write(k, cr)]
-                far = [k for c in cores for k in same(c) if k not in cores and topo.may_write(cq, k)
-                       and topo.may_write(k, cr)]
-                rest = [cores[t] for t in range(r, n) if not topo.may_write(cq, cores[t])]
-                h = min(own or far, key=lambda k: (-sum(topo.may_write(k, t) for t in rest), listed.get(k, 0),
-                                                   k not in relay))
-                listed[h] = listed.get(h, 0) + 1
-            hops.setdefault(h, []).append(cr)
-        if direct or hops:
-            flags.setdefault(cq, []).append((q, direct + list(hops)))
-        for h in hops:
-            flags.setdefault(h, []).append((q, hops[h]))
-    return flags, data, relay
+                good = [k for k in other if k in same(cq)] or [k for k in cand if k in same(cq)]
+                if not good:
+                    good = [k for k in other if topo.chip(k) == topo.chip(cr)]
+                    near = [k for k in good if rack(k) == rack(cq)]
+                    good = near or good
+            give(q, min(good or cand, key=lambda k: sum(topo.may_write(k, c) for c in cores)), r)
+    lists = {}
+    for (q, h) in hops:
+        lists.setdefault(cores[q], [(q, [])])[0][1].append(h)
+        lists[h] = [(q, [cores[hops[(q, h)]]])]
+    return lists, data, held
 
 
 def rank_program(g, core, T, topo):
     cores = list(T.cores)
     if "p" not in PLANS:
         PLANS["p"] = make_plan(cores, topo)
-    flags, data, relay = PLANS["p"]
+    lists, data, held = PLANS["p"]
     rank = T.rank_of(core)
-    if rank is None and core not in flags and core not in data:
+    if rank is None and core not in lists and core not in data:
         return
     S = T.sem
     sent = [0]
 
-    def fmask(c, dsts):
+    def lmask(c, dsts):
         m = topo.mask(c, dsts[0])
         for d in dsts[1:]:
             m &= topo.mask(c, d)
-        return part(m, 0, len(bits(m)) // 8)
+        return m
 
     def dstid(d):
         rid, pid = topo.addr(d, core)
@@ -150,11 +178,18 @@ def rank_program(g, core, T, topo):
     def nbits(m):
         return len(bits(m))
 
-    def send_flags(q, dsts):
-        m = fmask(core, dsts)
+    def place_of(q, d):
+        i = T.rank_of(d)
+        if i is None or (q, i) in held:
+            return T.fd[q]
+        c = LW * sum((p, i) not in held for p in range(q))
+        return T.ls[:, c:c + LW]
+
+    def send_list(q, dsts):
+        m = lmask(core, dsts)
         g.remote_dma_fused([RemoteDMATransfer(dst_ids=[dstid(d) for d in dsts], dma_engine_mask=m,
                                               remote_sem=S["f%d" % q], srcs=[T.fd[q]],
-                                              dsts=[T.fd[q] for d in dsts])], local_sem=S.snt)
+                                              dsts=[place_of(q, d) for d in dsts])], local_sem=S.snt)
         sent[0] += nbits(m)
 
     def send_data(call):
@@ -166,20 +201,16 @@ def rank_program(g, core, T, topo):
             sent[0] += nbits(m)
         g.remote_dma_fused(tr, local_sem=S.snt)
 
-    def flag_count(q, me):
-        for c in flags:
-            for (qq, dsts) in flags[c]:
-                if qq == q and me in dsts:
-                    return nbits(fmask(c, dsts))
-        return 0
+    def arrival(q, me):
+        return sum(nbits(lmask(c, dsts)) for c in lists for (p, dsts) in lists[c] if p == q and me in dsts)
 
     def landing(me, buf):
         return sum(nbits(t[6]) for c in data for call in data[c] for t in call if t[0] == me and t[3] == buf)
 
     if rank is None:
-        for (q, dsts) in flags.get(core, []):
-            g.wait_ge(S["f%d" % q], flag_count(q, core))
-            send_flags(q, dsts)
+        for (q, dsts) in lists.get(core, []):
+            g.wait_ge(S["f%d" % q], arrival(q, core))
+            send_list(q, dsts)
         if core in data:
             g.wait_ge(S.rarr, landing(core, "rb"))
             for call in data[core]:
@@ -193,12 +224,15 @@ def rank_program(g, core, T, topo):
     parts = min(r + 1, n - 1) - first + 1
     W = TC + SQ * parts
     own = TC + SQ * (r - first)
-    lo = 64 if r == 0 else 0
+    late = [q for q in range(r) if (q, r) in held]
+    swift = [q for q in range(r) if (q, r) not in held]
+    mid = 128 - LW * len(swift)
+    lo = mid - 64 if late else mid
     add, mx = AluOpType.add, AluOpType.max
 
     g.sync.dma_start(T.win[:, own:own + SQ], T.st[:]).then_inc(S.ldst, 16)
     g.sync.dma_start(T.win[:, 0:TC], T.x[:]).then_inc(S.ldx, 16)
-    if core in flags:
+    if core in lists:
         g.scalar.dma_start(T.fd[r], T.fl[:]).then_inc(S.ldfd, 16)
     g.scalar.dma_start(T.fo[:], T.fl[:]).then_inc(S.ldfo, 16)
 
@@ -207,15 +241,15 @@ def rank_program(g, core, T, topo):
     V.memset(T.big[:], BIG).then_inc(S.msk, 1)
     V.memset(T.ones[:], 1.0).then_inc(S.mone, 1)
     V.memset(T.ee[:, 0:1], 0.0).then_inc(S.mz, 1)
-    V.memset(T.d0[:, 0:64], 0.0).then_inc(S.mz, 1)
+    V.memset(T.d0[:, 0:128], 0.0).then_inc(S.mz, 1)
     g.iota(T.jv[:], [[256, 64]], 0, 1).then_inc(S.iot, 1)
     g.wait_ge(S.msk, 2)
     g.affine_select(T.lm[:], T.neg[:], [[0, 8], [-1, 16]], AluOpType.is_ge, 0.0, 0, 1).then_inc(S.aff, 1)
     g.affine_select(T.br[:], T.big[:], [[0, 8], [-1, 16]], AluOpType.is_equal, 0.0, 0, 1).then_inc(S.aff, 1)
 
-    for (q, dsts) in flags.get(core, []):
+    for (q, dsts) in lists.get(core, []):
         g.wait_ge(S.ldfd, 16)
-        send_flags(q, dsts)
+        send_list(q, dsts)
     g.wait_ge(S.ldst, 16)
     for call in data[core]:
         send_data(call)
@@ -234,28 +268,37 @@ def rank_program(g, core, T, topo):
     P.wait_ge(S.vfo, 1)
     P.matmul(T.psb[:, 0:64], T.lm[:], T.fob[:], True, False)
     P.matmul(T.psb[:, 0:64], T.br[:], T.fob[:], False, True).then_inc(S.pe1, 1)
-    P.matmul(T.psa[:, 64:128], T.ones[0:16, :], T.fob[:], True, True).then_inc(S.pe2, 1)
+    P.matmul(T.psa[:, 128:192], T.ones[0:16, :], T.fob[:], True, True).then_inc(S.pe2, 1)
     V.wait_ge(S.pe1, 1)
     V.tensor_scalar(T.ee[:, 1:65], T.psb[:, 0:64], float(TC - SQ * first) - BIG, None, add).then_inc(S.vee, 1)
     V.wait_ge(S.vee, 1)
     V.wait_ge(S.mz, 2)
-    V.tensor_tensor(T.d0[:, 64:128], T.ee[:, 1:65], T.ee[:, 0:64], AluOpType.subtract).then_inc(S.vd0, 1)
-
-    if r:
-        for q in range(r):
-            g.scalar.wait_ge(S["f%d" % q], flag_count(q, core))
-        g.scalar.dma_start(T.fp[0:16 * r, :], T.fd[0:r]).then_inc(S.ldfp, 16)
-        V.wait_ge(S.ldfp, 16)
-        V.tensor_copy(T.fpb[0:16 * r, :], T.fp[0:16 * r, :]).then_inc(S.vfp, 1)
-        P.wait_ge(S.vfp, 1)
-        P.matmul(T.psa[:, 0:64], T.ones[0:16 * r, :], T.fpb[0:16 * r, :], True, True).then_inc(S.pe3, 1)
-        V.wait_ge(S.pe3, 1)
+    V.tensor_tensor(T.d0[:, 128:192], T.ee[:, 1:65], T.ee[:, 0:64], AluOpType.subtract).then_inc(S.vd0, 1)
     V.wait_ge(S.pe2, 1)
     V.wait_ge(S.vd0, 1)
-    V.tensor_tensor_scan(T.us[:, lo:128], T.d0[:, lo:128], T.psa[:, lo:128], 0.0, add, add).then_inc(S.vus, 1)
-    V.wait_ge(S.vus, 1)
     V.wait_ge(S.vj, 1)
-    V.tensor_tensor(T.of[:], T.us[:, 64:128], T.jj[:], mx).then_inc(S.vof, 1)
+
+    K = 16 * len(late)
+    for i, q in enumerate(late):
+        g.scalar.wait_ge(S["f%d" % q], arrival(q, core))
+        g.scalar.dma_start(T.fp[16 * i:16 * (i + 1), :], T.fd[q]).then_inc(S.ldls, 16)
+    if swift:
+        for q in swift:
+            V.wait_ge(S["f%d" % q], arrival(q, core))
+        V.tensor_copy(T.lb[:, 0:LW * len(swift)], T.ls[:, 0:LW * len(swift)]).then_inc(S.vfp, 1)
+        P.wait_ge(S.vfp, 1)
+        P.matmul(T.psa[:, mid:128], T.ones[:], T.lb[:, 0:LW * len(swift)], True, True).then_inc(S.pe3, 1)
+    if late:
+        V.wait_ge(S.ldls, K)
+        V.tensor_copy(T.fpb[0:K, :], T.fp[0:K, :]).then_inc(S.vfq, 1)
+        P.wait_ge(S.vfq, 1)
+        P.matmul(T.psa[:, lo:mid], T.ones[0:K, :], T.fpb[0:K, :], True, True).then_inc(S.pe4, 1)
+        V.wait_ge(S.pe4, 1)
+    if swift:
+        V.wait_ge(S.pe3, 1)
+    V.tensor_tensor_scan(T.us[:, lo:192], T.d0[:, lo:192], T.psa[:, lo:192], 0.0, add, add).then_inc(S.vus, 1)
+    V.wait_ge(S.vus, 1)
+    V.tensor_tensor(T.of[:], T.us[:, 128:192], T.jj[:], mx).then_inc(S.vof, 1)
     V.wait_ge(S.vof, 1)
     V.tensor_copy(T.off[:], T.of[:]).then_inc(S.voff, 1)
 
@@ -264,14 +307,17 @@ def rank_program(g, core, T, topo):
         Q.wait_ge(S.ldst, 16)
         Q.wait_ge(S.ldx, 16)
         Q.wait_ge(S.darr, landing(core, "win"))
-    HT = TC // 2
-    V.tensor_copy(T.yb[:, 0:HT], T.win[:, 0:W].indirect(T.off[:, 0:32])).then_inc(S.gv, 1)
-    g.scalar.activation(T.yb[:, HT:TC], T.win[:, 0:W].indirect(T.off[:, 32:64]),
-                        ActivationFunctionType.Copy).then_inc(S.gs, 1)
-    g.sync.wait_ge(S.gv, 1)
-    g.sync.dma_start(T.y[:, 0:HT], T.yb[:, 0:HT]).then_inc(S.sty0, 16)
-    g.scalar.wait_ge(S.gs, 1)
-    g.scalar.dma_start(T.y[:, HT:TC], T.yb[:, HT:TC]).then_inc(S.sty1, 16)
+    a = 0
+    for i, b in enumerate((FIRST, TC)):
+        m = (a + b) // 2
+        V.tensor_copy(T.yb[:, a:m], T.win[:, 0:W].indirect(T.off[:, a // 16:m // 16])).then_inc(S["gv%d" % i], 1)
+        g.scalar.activation(T.yb[:, m:b], T.win[:, 0:W].indirect(T.off[:, m // 16:b // 16]),
+                            ActivationFunctionType.Copy).then_inc(S["gs%d" % i], 1)
+        Q = g.sync if b < TC else g.scalar
+        Q.wait_ge(S["gv%d" % i], 1)
+        Q.wait_ge(S["gs%d" % i], 1)
+        Q.dma_start(T.y[:, a:b], T.yb[:, a:b]).then_inc(S["sty%d" % i], 16)
+        a = b
     g.sync.wait_ge(S.sty0, 16)
     g.scalar.wait_ge(S.sty1, 16)
     g.wait_ge(S.snt, sent[0])

@@ -8,6 +8,9 @@ NR = 8
 BIG = 8192.0
 LW = 8
 FIRST = 256
+FAN = 4
+RC = 144
+RU = 176
 
 SCRATCH = {
     "win": ("sbuf", [128, TC + 3 * SQ], "float32"),
@@ -61,73 +64,79 @@ def make_plan(cores, topo):
     same = lambda a: place[(topo.host(a), topo.chip(a))]
     rack = lambda k: topo.rack(topo.host(k))
     n = len(cores)
-    H = SQ // 2
 
     data, stream = {}, {}
 
     def base(r, p):
         return TC + SQ * (p - max(r - 1, 0))
 
-    def idle(c):
-        return [k for k in same(c) if k not in cores and k not in stream]
+    def piece(s, d, o, w, m):
+        return (cores[d], "win", base(s, s) + o, "win", base(d, s) + o, w, m)
+
+    def via(h, s, d, o, w, m):
+        stream[h] = s
+        data[h] = [[(cores[d], "rb", 0, "win", base(d, s) + o, w, topo.mask(h, cores[d]))]]
+        return (h, "win", base(s, s) + o, "rb", 0, w, m)
 
     for s in range(n):
-        relayed, plane = [], []
         cs = cores[s]
-
-        def via(h, d, o, m):
-            stream[h] = s
-            data[h] = [[(cores[d], "rb", 0, "win", base(d, s) + o, H, topo.mask(h, cores[d]))]]
-            return (h, "win", base(s, s) + o, "rb", 0, H, m)
-
-        for d in (s - 1, s + 1):
-            if not 0 <= d < n:
-                continue
+        near = [d for d in (s - 1, s + 1) if 0 <= d < n]
+        plane = [d for d in near if topo.same_plane(cs, cores[d])][0]
+        out = topo.mask(cs, cores[plane])
+        data[cs] = []
+        for d in [d for d in near if d != plane]:
             cd = cores[d]
-            so, do = base(s, s), base(d, s)
-            if topo.may_write(cs, cd) and topo.same_plane(cs, cd):
-                plane.append([(cd, "win", so, "win", do, SQ, topo.mask(cs, cd))])
-            elif topo.may_write(cs, cd):
-                h = [k for k in idle(cs) if topo.may_write(k, cd) and topo.die(k) != topo.die(cs)
-                     and any(topo.may_write(k, c) for c in cores if not topo.may_write(cs, c))][0]
-                relayed.append([via(h, d, H, topo.mask(cs, h) & ~topo.mask(cs, cd)),
-                                (cd, "win", so, "win", do, H, topo.mask(cs, cd))])
+            straight = topo.may_write(cs, cd)
+            w = RC if straight else RU
+            own = [k for k in same(cs) if k not in cores and topo.may_write(k, cd)
+                   and any(topo.may_write(k, c) and not topo.may_write(cs, c) for c in cores)]
+            hs = [[k for k in own if topo.die(k) == e][0] for e in (0, 1)]
+            on = topo.mask(cs, hs[0]) & ~out
+            data[cs].append([via(h, s, d, i * w, w, part(on, i, 2)) for i, h in enumerate(hs)])
+            if straight:
+                data[cs].append([piece(s, d, 2 * w, SQ - 2 * w, part(out, 0, 2))])
             else:
-                h0, h1 = [[k for k in idle(cs) if topo.may_write(k, cd) and topo.die(k) == e][0] for e in (0, 1)]
-                on = topo.mask(cs, h0)
-                relayed.append([via(h0, d, 0, part(on, 1, 2)), via(h1, d, H, part(on, 0, 2))])
-        data[cs] = relayed + plane
+                far = [k for k in range(total) if topo.host(k) == topo.host(cd) and topo.chip(k) == topo.chip(cs)
+                       and k not in cores and k not in stream and topo.may_write(cs, k) and topo.may_write(k, cd)
+                       and topo.die(k) != topo.die(cs)][0]
+                data[cs].append([via(far, s, d, 2 * w, SQ - 2 * w, topo.mask(cs, far))])
+        beside_cable = any(topo.may_write(cs, cores[d]) for d in near if d != plane)
+        data[cs].append([piece(s, plane, 0, SQ, part(out, 1, 2) if beside_cable else out)])
 
     hops, jobs = {}, set()
-    held = set()
+    held, done = set(), set()
     last = n - 1
 
     def give(q, h, r):
         hops[(q, h)] = r
         jobs.add(h)
+        done.add((q, r))
 
     def beside(k, r):
         return topo.mates(k, place[(topo.host(k), topo.chip(cores[r]))][0])
 
-    odd = [h for h in stream if not topo.may_write(cores[stream[h]], data[h][0][0][0])]
+    def choose(h, key, ok):
+        can = [(q, r) for q in range(n) for r in range(q + 1, n) if (q, r) not in done and ok(q, r)
+               and topo.may_write(cores[q], h) and topo.may_write(h, cores[r])]
+        return min(can, key=key) if can else None
+
+    odd = [h for h in stream if h in same(cores[stream[h]]) and not topo.may_write(cores[stream[h]], data[h][0][0][0])]
     for h in odd:
-        can = [q for q in range(last) if (q, last) not in held and topo.may_write(cores[q], h)
-               and topo.may_write(h, cores[last])]
-        can.sort(key=lambda q: (q != stream[h], rack(cores[q]) != rack(h), -q))
-        if can:
-            give(can[0], h, last)
-            held.add((can[0], last))
+        x = choose(h, lambda x: (x[0] != stream[h], rack(cores[x[0]]) != rack(h), -x[0]), lambda q, r: r == last)
+        if x:
+            give(x[0], h, x[1])
+            held.add(x)
+    for h in sorted([h for h in stream if h not in odd], key=lambda h: (h in same(cores[stream[h]]), stream[h])):
+        goal = topo.host(data[h][0][0][0])
+        x = choose(h, lambda x: (topo.host(cores[x[1]]) != goal, topo.may_write(cores[x[0]], cores[x[1]])),
+                   lambda q, r: q == stream[h])
+        x = x or choose(h, lambda x: (topo.host(cores[x[0]]) != topo.host(h), rack(cores[x[0]]) != rack(h),
+                                      topo.host(cores[x[1]]) != topo.host(h)), lambda q, r: True)
+        if x:
+            give(x[0], h, x[1])
     for q in range(n):
         cq = cores[q]
-        todo = [r for r in range(q + 1, n) if (q, r) not in held]
-        for h in [h for h in stream if stream[h] == q and h not in jobs]:
-            goal = topo.host(data[h][0][0][0])
-            can = [r for r in todo if topo.may_write(h, cores[r])]
-            can.sort(key=lambda r: (topo.host(cores[r]) != goal, topo.may_write(cq, cores[r])))
-            if can:
-                give(q, h, can[0])
-                todo.remove(can[0])
-        for r in todo:
+        for r in [r for r in range(q + 1, n) if (q, r) not in done]:
             cr = cores[r]
             cand = [k for p in place.values() for k in p if k not in cores and k not in stream and k not in jobs
                     and topo.may_write(cq, k) and topo.may_write(k, cr)]
@@ -165,11 +174,14 @@ def rank_program(g, core, T, topo):
     S = T.sem
     sent = [0]
 
-    def lmask(c, dsts):
+    def groups(c, dsts):
+        k = 1
+        while k < min(len(dsts), FAN):
+            k *= 2
         m = topo.mask(c, dsts[0])
         for d in dsts[1:]:
             m &= topo.mask(c, d)
-        return m
+        return [(part(m, i, k), dsts[i::k]) for i in range(k) if dsts[i::k]]
 
     def dstid(d):
         rid, pid = topo.addr(d, core)
@@ -186,11 +198,12 @@ def rank_program(g, core, T, topo):
         return T.ls[:, c:c + LW]
 
     def send_list(q, dsts):
-        m = lmask(core, dsts)
-        g.remote_dma_fused([RemoteDMATransfer(dst_ids=[dstid(d) for d in dsts], dma_engine_mask=m,
-                                              remote_sem=S["f%d" % q], srcs=[T.fd[q]],
-                                              dsts=[place_of(q, d) for d in dsts])], local_sem=S.snt)
-        sent[0] += nbits(m)
+        tr = []
+        for m, ds in groups(core, dsts):
+            tr.append(RemoteDMATransfer(dst_ids=[dstid(d) for d in ds], dma_engine_mask=m, remote_sem=S["f%d" % q],
+                                        srcs=[T.fd[q]], dsts=[place_of(q, d) for d in ds]))
+            sent[0] += nbits(m)
+        g.remote_dma_fused(tr, local_sem=S.snt)
 
     def send_data(call):
         tr = []
@@ -202,7 +215,8 @@ def rank_program(g, core, T, topo):
         g.remote_dma_fused(tr, local_sem=S.snt)
 
     def arrival(q, me):
-        return sum(nbits(lmask(c, dsts)) for c in lists for (p, dsts) in lists[c] if p == q and me in dsts)
+        return sum(nbits(m) for c in lists for (p, dsts) in lists[c] if p == q
+                   for m, ds in groups(c, dsts) if me in ds)
 
     def landing(me, buf):
         return sum(nbits(t[6]) for c in data for call in data[c] for t in call if t[0] == me and t[3] == buf)

import numpy as np
from concourse.bass import DstId, RemoteDMATransfer
from concourse.mybir import dt, AluOpType, AxisListType, ActivationFunctionType

TC = 1024
SQ = 512
NR = 8
BIG = 8192.0
LW = 8
FIRST = 256
FAN = 4
RC = 144
RU = 176

SCRATCH = {
    "win": ("sbuf", [128, TC + 3 * SQ], "float32"),
    "yb": ("sbuf", [128, TC], "float32"),
    "rb": ("sbuf", [128, SQ // 2], "float32"),
    "fd": ("dram", [NR, 128, LW], "int32"),
    "ls": ("sbuf", [128, LW * NR], "int32"),
    "lb": ("sbuf", [128, LW * NR], "bfloat16"),
    "fp": ("sbuf", [128, 64], "int32"),
    "fpb": ("sbuf", [128, 64], "bfloat16"),
    "fo": ("sbuf", [16, 64], "int32"),
    "fob": ("sbuf", [16, 64], "bfloat16"),
    "ones": ("sbuf", [128, 128], "bfloat16"),
    "neg": ("sbuf", [16, 128], "bfloat16"),
    "big": ("sbuf", [16, 128], "bfloat16"),
    "lm": ("sbuf", [16, 128], "bfloat16"),
    "br": ("sbuf", [16, 128], "bfloat16"),
    "jv": ("sbuf", [128, 64], "int32"),
    "ja": ("sbuf", [128, 64], "int32"),
    "jb": ("sbuf", [128, 64], "int32"),
    "jj": ("sbuf", [128, 64], "float32"),
    "ee": ("sbuf", [128, 65], "float32"),
    "d0": ("sbuf", [128, 192], "float32"),
    "us": ("sbuf", [128, 192], "float32"),
    "of": ("sbuf", [128, 64], "float32"),
    "off": ("sbuf", [128, 64], "uint16"),
    "psa": ("psum", [128, 512], "float32"),
    "psb": ("psum", [128, 512], "float32"),
}
SEMAPHORES = (["f%d" % q for q in range(NR)]
              + ["ldfd", "ldfo", "ldst", "ldx", "ldls", "darr", "rarr", "snt", "msk", "mone", "mz", "aff", "iot",
                 "vj1", "vj2", "vj", "vfo", "pe1", "pe2", "vee", "vd0", "vfp", "vfq", "pe3", "pe4", "vus", "vof",
                 "voff", "gv0", "gs0", "gv1", "gs1", "sty0", "sty1"])

PLANS = {}


def bits(mask):
    return [1 << i for i in range(16) if (mask >> i) & 1]


def part(mask, k, n):
    return sum(bits(mask)[k::n])


def make_plan(cores, topo):
    total = topo.CORES_PER_HOST * (1 + max(topo.host(c) for c in cores))
    place = {}
    for k in range(total):
        place.setdefault((topo.host(k), topo.chip(k)), []).append(k)
    same = lambda a: place[(topo.host(a), topo.chip(a))]
    rack = lambda k: topo.rack(topo.host(k))
    n = len(cores)

    data, stream = {}, {}

    def base(r, p):
        return TC + SQ * (p - max(r - 1, 0))

    def piece(s, d, o, w, m):
        return (cores[d], "win", base(s, s) + o, "win", base(d, s) + o, w, m)

    def via(h, s, d, o, w, m):
        stream[h] = s
        data[h] = [[(cores[d], "rb", 0, "win", base(d, s) + o, w, topo.mask(h, cores[d]))]]
        return (h, "win", base(s, s) + o, "rb", 0, w, m)

    for s in range(n):
        cs = cores[s]
        near = [d for d in (s - 1, s + 1) if 0 <= d < n]
        plane = [d for d in near if topo.same_plane(cs, cores[d])][0]
        out = topo.mask(cs, cores[plane])
        data[cs] = []
        for d in [d for d in near if d != plane]:
            cd = cores[d]
            straight = topo.may_write(cs, cd)
            w = RC if straight else RU
            own = [k for k in same(cs) if k not in cores and topo.may_write(k, cd)
                   and any(topo.may_write(k, c) and not topo.may_write(cs, c) for c in cores)]
            hs = [[k for k in own if topo.die(k) == e][0] for e in (0, 1)]
            on = topo.mask(cs, hs[0]) & ~out
            data[cs].append([via(h, s, d, i * w, w, part(on, i, 2)) for i, h in enumerate(hs)])
            if straight:
                data[cs].append([piece(s, d, 2 * w, SQ - 2 * w, part(out, 0, 2))])
            else:
                far = [k for k in range(total) if topo.host(k) == topo.host(cd) and topo.chip(k) == topo.chip(cs)
                       and k not in cores and k not in stream and topo.may_write(cs, k) and topo.may_write(k, cd)
                       and topo.die(k) != topo.die(cs)][0]
                data[cs].append([via(far, s, d, 2 * w, SQ - 2 * w, topo.mask(cs, far))])
        beside_cable = any(topo.may_write(cs, cores[d]) for d in near if d != plane)
        data[cs].append([piece(s, plane, 0, SQ, part(out, 1, 2) if beside_cable else out)])

    hops, jobs = {}, set()
    held, done = set(), set()
    last = n - 1

    def give(q, h, r):
        hops[(q, h)] = r
        jobs.add(h)
        done.add((q, r))

    def beside(k, r):
        return topo.mates(k, place[(topo.host(k), topo.chip(cores[r]))][0])

    def choose(h, key, ok):
        can = [(q, r) for q in range(n) for r in range(q + 1, n) if (q, r) not in done and ok(q, r)
               and topo.may_write(cores[q], h) and topo.may_write(h, cores[r])]
        return min(can, key=key) if can else None

    odd = [h for h in stream if h in same(cores[stream[h]]) and not topo.may_write(cores[stream[h]], data[h][0][0][0])]
    for h in odd:
        x = choose(h, lambda x: (x[0] != stream[h], rack(cores[x[0]]) != rack(h), -x[0]), lambda q, r: r == last)
        if x:
            give(x[0], h, x[1])
            held.add(x)
    for h in sorted([h for h in stream if h not in odd], key=lambda h: (h in same(cores[stream[h]]), stream[h])):
        goal = topo.host(data[h][0][0][0])
        x = choose(h, lambda x: (topo.host(cores[x[1]]) != goal, topo.may_write(cores[x[0]], cores[x[1]])),
                   lambda q, r: q == stream[h])
        x = x or choose(h, lambda x: (topo.host(cores[x[0]]) != topo.host(h), rack(cores[x[0]]) != rack(h),
                                      topo.host(cores[x[1]]) != topo.host(h)), lambda q, r: True)
        if x:
            give(x[0], h, x[1])
    for q in range(n):
        cq = cores[q]
        for r in [r for r in range(q + 1, n) if (q, r) not in done]:
            cr = cores[r]
            cand = [k for p in place.values() for k in p if k not in cores and k not in stream and k not in jobs
                    and topo.may_write(cq, k) and topo.may_write(k, cr)]
            other = [k for k in cand if topo.die(k) != topo.die(cq)]
            if topo.chip(cq) != topo.chip(cr):
                if topo.host(cr) == topo.host(cq):
                    good = [k for k in other if topo.mates(k, cr)]
                else:
                    good = [k for k in other if k in same(cq) and not any(h in same(cq) for h in odd)]
                    good = good or [k for k in other if topo.mates(k, cr)]
                good = good or [k for k in other if beside(k, r) and rack(k) == rack(cr)]
                good = good or [k for k in cand if beside(k, r) and rack(k) == rack(cq)]
            else:
                good = [k for k in other if k in same(cq)] or [k for k in cand if k in same(cq)]
                if not good:
                    good = [k for k in other if topo.chip(k) == topo.chip(cr)]
                    near = [k for k in good if rack(k) == rack(cq)]
                    good = near or good
            give(q, min(good or cand, key=lambda k: sum(topo.may_write(k, c) for c in cores)), r)
    lists = {}
    for (q, h) in hops:
        lists.setdefault(cores[q], [(q, [])])[0][1].append(h)
        lists[h] = [(q, [cores[hops[(q, h)]]])]
    return lists, data, held


def rank_program(g, core, T, topo):
    cores = list(T.cores)
    if "p" not in PLANS:
        PLANS["p"] = make_plan(cores, topo)
    lists, data, held = PLANS["p"]
    rank = T.rank_of(core)
    if rank is None and core not in lists and core not in data:
        return
    S = T.sem
    sent = [0]

    def groups(c, dsts):
        k = 1
        while k < min(len(dsts), FAN):
            k *= 2
        m = topo.mask(c, dsts[0])
        for d in dsts[1:]:
            m &= topo.mask(c, d)
        return [(part(m, i, k), dsts[i::k]) for i in range(k) if dsts[i::k]]

    def dstid(d):
        rid, pid = topo.addr(d, core)
        return DstId(rid=rid, pnc=pid)

    def nbits(m):
        return len(bits(m))

    def place_of(q, d):
        i = T.rank_of(d)
        if i is None or (q, i) in held:
            return T.fd[q]
        c = LW * sum((p, i) not in held for p in range(q))
        return T.ls[:, c:c + LW]

    def send_list(q, dsts):
        tr = []
        for m, ds in groups(core, dsts):
            tr.append(RemoteDMATransfer(dst_ids=[dstid(d) for d in ds], dma_engine_mask=m, remote_sem=S["f%d" % q],
                                        srcs=[T.fd[q]], dsts=[place_of(q, d) for d in ds]))
            sent[0] += nbits(m)
        g.remote_dma_fused(tr, local_sem=S.snt)

    def send_data(call):
        tr = []
        for (d, sb, sc, db, dc, w, m) in call:
            tr.append(RemoteDMATransfer(dst_ids=[dstid(d)], dma_engine_mask=m,
                                        remote_sem=S["darr" if db == "win" else "rarr"],
                                        srcs=[T[sb][:, sc:sc + w]], dsts=[T[db][:, dc:dc + w]]))
            sent[0] += nbits(m)
        g.remote_dma_fused(tr, local_sem=S.snt)

    def arrival(q, me):
        return sum(nbits(m) for c in lists for (p, dsts) in lists[c] if p == q
                   for m, ds in groups(c, dsts) if me in ds)

    def landing(me, buf):
        return sum(nbits(t[6]) for c in data for call in data[c] for t in call if t[0] == me and t[3] == buf)

    if rank is None:
        for (q, dsts) in lists.get(core, []):
            g.wait_ge(S["f%d" % q], arrival(q, core))
            send_list(q, dsts)
        if core in data:
            g.wait_ge(S.rarr, landing(core, "rb"))
            for call in data[core]:
                send_data(call)
        g.wait_ge(S.snt, sent[0])
        return

    r = rank
    n = len(cores)
    first = max(r - 1, 0)
    parts = min(r + 1, n - 1) - first + 1
    W = TC + SQ * parts
    own = TC + SQ * (r - first)
    late = [q for q in range(r) if (q, r) in held]
    swift = [q for q in range(r) if (q, r) not in held]
    mid = 128 - LW * len(swift)
    lo = mid - 64 if late else mid
    add, mx = AluOpType.add, AluOpType.max

    g.sync.dma_start(T.win[:, own:own + SQ], T.st[:]).then_inc(S.ldst, 16)
    g.sync.dma_start(T.win[:, 0:TC], T.x[:]).then_inc(S.ldx, 16)
    if core in lists:
        g.scalar.dma_start(T.fd[r], T.fl[:]).then_inc(S.ldfd, 16)
    g.scalar.dma_start(T.fo[:], T.fl[:]).then_inc(S.ldfo, 16)

    V = g.vector
    V.memset(T.neg[:], -1.0).then_inc(S.msk, 1)
    V.memset(T.big[:], BIG).then_inc(S.msk, 1)
    V.memset(T.ones[:], 1.0).then_inc(S.mone, 1)
    V.memset(T.ee[:, 0:1], 0.0).then_inc(S.mz, 1)
    V.memset(T.d0[:, 0:128], 0.0).then_inc(S.mz, 1)
    g.iota(T.jv[:], [[256, 64]], 0, 1).then_inc(S.iot, 1)
    g.wait_ge(S.msk, 2)
    g.affine_select(T.lm[:], T.neg[:], [[0, 8], [-1, 16]], AluOpType.is_ge, 0.0, 0, 1).then_inc(S.aff, 1)
    g.affine_select(T.br[:], T.big[:], [[0, 8], [-1, 16]], AluOpType.is_equal, 0.0, 0, 1).then_inc(S.aff, 1)

    for (q, dsts) in lists.get(core, []):
        g.wait_ge(S.ldfd, 16)
        send_list(q, dsts)
    g.wait_ge(S.ldst, 16)
    for call in data[core]:
        send_data(call)

    V.wait_ge(S.iot, 1)
    V.tensor_scalar(T.ja[:], T.jv[:], 15, None, AluOpType.bitwise_and).then_inc(S.vj1, 1)
    V.tensor_scalar(T.jb[:], T.jv[:], 4, 1008, AluOpType.arith_shift_right, AluOpType.bitwise_and).then_inc(S.vj2, 1)
    V.wait_ge(S.vj1, 1)
    V.wait_ge(S.vj2, 1)
    V.tensor_tensor(T.jj[:], T.ja[:], T.jb[:], add).then_inc(S.vj, 1)
    V.wait_ge(S.ldfo, 16)
    V.tensor_copy(T.fob[:], T.fo[:]).then_inc(S.vfo, 1)
    P = g.tensor
    P.wait_ge(S.mone, 1)
    P.wait_ge(S.aff, 2)
    P.wait_ge(S.vfo, 1)
    P.matmul(T.psb[:, 0:64], T.lm[:], T.fob[:], True, False)
    P.matmul(T.psb[:, 0:64], T.br[:], T.fob[:], False, True).then_inc(S.pe1, 1)
    P.matmul(T.psa[:, 128:192], T.ones[0:16, :], T.fob[:], True, True).then_inc(S.pe2, 1)
    V.wait_ge(S.pe1, 1)
    V.tensor_scalar(T.ee[:, 1:65], T.psb[:, 0:64], float(TC - SQ * first) - BIG, None, add).then_inc(S.vee, 1)
    V.wait_ge(S.vee, 1)
    V.wait_ge(S.mz, 2)
    V.tensor_tensor(T.d0[:, 128:192], T.ee[:, 1:65], T.ee[:, 0:64], AluOpType.subtract).then_inc(S.vd0, 1)
    V.wait_ge(S.pe2, 1)
    V.wait_ge(S.vd0, 1)
    V.wait_ge(S.vj, 1)

    K = 16 * len(late)
    for i, q in enumerate(late):
        g.scalar.wait_ge(S["f%d" % q], arrival(q, core))
        g.scalar.dma_start(T.fp[16 * i:16 * (i + 1), :], T.fd[q]).then_inc(S.ldls, 16)
    if swift:
        for q in swift:
            V.wait_ge(S["f%d" % q], arrival(q, core))
        V.tensor_copy(T.lb[:, 0:LW * len(swift)], T.ls[:, 0:LW * len(swift)]).then_inc(S.vfp, 1)
        P.wait_ge(S.vfp, 1)
        P.matmul(T.psa[:, mid:128], T.ones[:], T.lb[:, 0:LW * len(swift)], True, True).then_inc(S.pe3, 1)
    if late:
        V.wait_ge(S.ldls, K)
        V.tensor_copy(T.fpb[0:K, :], T.fp[0:K, :]).then_inc(S.vfq, 1)
        P.wait_ge(S.vfq, 1)
        P.matmul(T.psa[:, lo:mid], T.ones[0:K, :], T.fpb[0:K, :], True, True).then_inc(S.pe4, 1)
        V.wait_ge(S.pe4, 1)
    if swift:
        V.wait_ge(S.pe3, 1)
    V.tensor_tensor_scan(T.us[:, lo:192], T.d0[:, lo:192], T.psa[:, lo:192], 0.0, add, add).then_inc(S.vus, 1)
    V.wait_ge(S.vus, 1)
    V.tensor_tensor(T.of[:], T.us[:, 128:192], T.jj[:], mx).then_inc(S.vof, 1)
    V.wait_ge(S.vof, 1)
    V.tensor_copy(T.off[:], T.of[:]).then_inc(S.voff, 1)

    for Q in (V, g.scalar):
        Q.wait_ge(S.voff, 1)
        Q.wait_ge(S.ldst, 16)
        Q.wait_ge(S.ldx, 16)
        Q.wait_ge(S.darr, landing(core, "win"))
    a = 0
    for i, b in enumerate((FIRST, TC)):
        m = (a + b) // 2
        V.tensor_copy(T.yb[:, a:m], T.win[:, 0:W].indirect(T.off[:, a // 16:m // 16])).then_inc(S["gv%d" % i], 1)
        g.scalar.activation(T.yb[:, m:b], T.win[:, 0:W].indirect(T.off[:, m // 16:b // 16]),
                            ActivationFunctionType.Copy).then_inc(S["gs%d" % i], 1)
        Q = g.sync if b < TC else g.scalar
        Q.wait_ge(S["gv%d" % i], 1)
        Q.wait_ge(S["gs%d" % i], 1)
        Q.dma_start(T.y[:, a:b], T.yb[:, a:b]).then_inc(S["sty%d" % i], 16)
        a = b
    g.sync.wait_ge(S.sty0, 16)
    g.scalar.wait_ge(S.sty1, 16)
    g.wait_ge(S.snt, sent[0])
